import numpy as np
import ml_dtypes


def mxq(x, axis, fmt="e4m3"):
    dtype, down = {"e4m3": (ml_dtypes.float8_e4m3fn, 7), "e5m2": (ml_dtypes.float8_e5m2, 14)}[fmt]
    v = np.moveaxis(np.asarray(x, np.float32).astype(ml_dtypes.bfloat16).astype(np.float64), axis, -1)
    blocks = v.reshape(v.shape[:-1] + (-1, 32))
    amax = np.abs(blocks).max(-1, keepdims=True)
    byte = np.maximum(np.where(amax > 0, np.frexp(amax)[1] - 1 + 127, 0) - down, 1)
    scale = np.exp2(byte - 127.0)
    codes = (blocks / scale).astype(np.float32).astype(dtype).astype(np.float64)
    return np.moveaxis((codes * scale).reshape(v.shape), -1, axis)


WIDE = False


def mx_kscale(k):
    if not WIDE:
        return np.ones(k)
    levels = np.array([10, -10, 5, -5, 0])
    if k % 512:
        return np.exp2(np.random.permutation(np.resize(levels, k // 32))).repeat(32)
    a = np.empty((k // 512, 16))
    for p in range(k // 512):
        a[p, :8] = np.random.permutation(np.resize(levels, 8))
        for g in range(8):
            far = levels[np.abs(levels - a[p, g]) >= 10]
            a[p, g + 8] = far[np.random.randint(len(far))]
    return np.exp2(a.ravel()).repeat(32)


def f64(x):
    return np.asarray(x).astype(np.float64)


def striped(idx):
    return np.tile(idx.reshape(-1, 16).T, (8, 1)).astype(np.uint16)


def unstriped(offs):
    return offs[:16].T.reshape(-1).astype(np.int64)


E2M1 = np.array([0.0, 0.5, 1.0, 1.5, 2.0, 3.0, 4.0, 6.0, -0.0, -0.5, -1.0, -1.5, -2.0, -3.0, -4.0, -6.0])


def pack_weight(w, fmt):
    k, n = w.shape
    w = f64(np.asarray(w, np.float32).astype(ml_dtypes.bfloat16)).reshape(k // 32, 32, n)
    amax = np.abs(w).max(1)
    if fmt == "e4m3":
        byte = np.frexp(amax)[1] - 1 + 127 - 7
    else:
        mant, ex = np.frexp(amax / 6.0)
        byte = np.where(mant > 0.5, ex, ex - 1) + 127
    byte = np.clip(np.where(amax > 0, byte, 1), 1, 254)
    scaled = (w * np.exp2(127.0 - byte)[:, None, :]).reshape(k, n).astype(np.float32)
    by_word = np.ascontiguousarray(scaled.reshape(k // 512, 128, 4, n).transpose(0, 1, 3, 2))
    if fmt == "e4m3":
        words = by_word.astype(ml_dtypes.float8_e4m3fn).view(np.uint8)
    else:
        c = by_word.astype(ml_dtypes.float4_e2m1fn).view(np.uint8) & 0xF
        words = (c[..., 0::2] | (c[..., 1::2] << 4)).reshape(k // 512, 128, 2 * n)
    return np.ascontiguousarray(words), np.ascontiguousarray(byte.astype(np.uint8).reshape(k // 512, 16, n))


def unpack_weight(words, scales, fmt):
    g, _, n = scales.shape
    words = np.ascontiguousarray(words).reshape(g, 128, n, -1)
    if fmt == "e4m3":
        vals = words.view(ml_dtypes.float8_e4m3fn).astype(np.float64)
    else:
        nib = np.empty((g, 128, n, 4), np.uint8)
        nib[..., 0::2] = words & 0xF
        nib[..., 1::2] = words >> 4
        vals = E2M1[nib]
    vals = vals * np.repeat(np.exp2(scales.astype(np.float64) - 127.0), 8, axis=1)[..., None]
    return vals.transpose(0, 1, 3, 2).reshape(g * 512, n)


def gelu(v):
    return 0.5 * v * (1.0 + np.tanh(np.sqrt(2.0 / np.pi) * (v + 0.044715 * v**3)))


K, H, N, T, S, T2 = 1536, 512, 768, 2048, 1024, 2048

def setup_inputs():
    n = np.random.standard_normal
    s = mx_kscale(K)[:, None]
    u = mx_kscale(H)[:, None]
    tab_words, tab_scales = pack_weight(n((K, T)) * s, "e4m3")
    wa = 0.55 / np.sqrt(K) * n((K, H)) / s
    wb_words, wb_scales = pack_weight(0.55 / np.sqrt(K) * n((K, H)) / s, "e2m1")
    wc_words, wc_scales = pack_weight(1.2 / np.sqrt(H) * n((H, N)) / u, "e2m1")
    we = 2.2 / np.sqrt(H) * n((H, N)) / u
    return {
        "tab_words": tab_words, "tab_scales": tab_scales,
        "offs": striped(np.random.permutation(T)[:S]),
        "offs2": striped(np.random.permutation(T)[:S]),
        "offs3": striped(np.random.permutation(T2)[:S]),
        "wa": wa.astype(np.float32),
        "wb_words": wb_words, "wb_scales": wb_scales,
        "wc_words": wc_words, "wc_scales": wc_scales,
        "we": we.astype(np.float32),
        "gmax": (np.exp(0.3 * n(H)) * u[:, 0]).astype(np.float32),
        "gwave": (np.exp(0.3 * n(H)) * u[:, 0]).astype(np.float32),
        "wgo": np.exp(0.3 * n((128, S))).astype(np.float32),
    }

def reference(tab_words, tab_scales, offs, offs2, offs3, wa, wb_words, wb_scales,
              wc_words, wc_scales, we, gmax, gwave, wgo):
    TW = unpack_weight(tab_words, tab_scales, "e4m3")
    v = TW[:, unstriped(offs)]
    v2 = TW[:, unstriped(offs2)]
    a = mxq(f64(wa), 0, "e4m3").T @ v
    b = unpack_weight(wb_words, wb_scales, "e2m1").T @ v2
    z1 = np.maximum(a, b) * f64(gmax)[:, None]
    z2 = np.sin(a) * np.cos(b) * f64(gwave)[:, None]
    wc = unpack_weight(wc_words, wc_scales, "e2m1")
    y = np.tanh(wc.T @ mxq(z1, 0, "e4m3")
                      + mxq(f64(we), 0, "e4m3").T @ mxq(z2, 0, "e4m3"))
    out = np.zeros((N, T2))
    out[:, unstriped(offs3)] = np.tile(f64(wgo), (N // 128, 1)) * y
    return out

@@ -1,0 +1,304 @@
+import math
+from contextlib import ExitStack
+
+import concourse.mybir as mybir
+from concourse.masks import make_identity
+
+K, H, N, T, S, T2 = 1536, 512, 768, 2048, 1024, 2048
+FLOPS = 2 * (2 * K * H * S + 2 * H * N * S)
+
+F32 = mybir.dt.float32
+BF16 = mybir.dt.bfloat16
+I32 = mybir.dt.int32
+U32 = mybir.dt.uint32
+U16 = mybir.dt.uint16
+U8 = mybir.dt.uint8
+FP8X4 = mybir.dt.float8_e4m3fn_x4
+FP4X4 = mybir.dt.float4_e2m1fn_x4
+ACT = mybir.ActivationFunctionType
+ALU = mybir.AluOpType
+
+P = 128
+PACK = 4
+PASSES = K // (P * PACK)
+BLOCK = 128
+CHUNK = 256
+ROW_BLOCKS = N // P
+WE_HALF = N // 2
+CHUNKS = S // CHUNK
+GATHER_AHEAD = 2
+TURN = 2.0 * math.pi
+ANCHOR = 98304.0
+ANCHOR_BITS = 1203765248.0
+ULPS_PER_TURN = 128.0
+
+
+def tile_list_mesh_link_features_kernel(
+    tc, tab_words, tab_scales, offs, offs2, offs3, wa, wb_words, wb_scales,
+    wc_words, wc_scales, we, gmax, gwave, wgo, out,
+):
+    nc = tc.nc
+    with ExitStack() as ctx:
+        keep = ctx.enter_context(tc.tile_pool(name="keep", bufs=1))
+        stage = ctx.enter_context(tc.tile_pool(name="stage", bufs=2))
+        work = ctx.enter_context(tc.tile_pool(name="work", bufs=2))
+        psum = ctx.enter_context(tc.psum_pool(name="psum", bufs=1))
+
+        list_a = keep.tile([P, S // 16], U16, name="list_a")
+        list_b = keep.tile([P, S // 16], U16, name="list_b")
+        list_out = keep.tile([P, S // 16], U16, name="list_out")
+        table = [keep.tile([P, T], I32, name="table%d" % a, align_bytes=64) for a in range(PASSES)]
+        table_scales = keep.tile([P, T], U8, name="table_scales", align_bytes=64)
+        v2_scales = [keep.tile([P, S], U8, name="v2_scales%d" % a, align_bytes=64) for a in range(PASSES)]
+        wa_codes = [keep.tile([P, H], U32, name="wa_codes%d" % a, align_bytes=64) for a in range(PASSES)]
+        wa_scales = [keep.tile([P, H], U8, name="wa_scales%d" % a, align_bytes=64) for a in range(PASSES)]
+        wb_sb = keep.tile([P, PASSES, 2 * H], U8, name="wb_sb", align_bytes=64)
+        wb_scales_sb = keep.tile([P, PASSES, H], U8, name="wb_scales_sb", align_bytes=64)
+        wc_sb = keep.tile([P, 2 * N], U8, name="wc_sb", align_bytes=64)
+        wc_scales_sb = keep.tile([P, N], U8, name="wc_scales_sb", align_bytes=64)
+        we_codes = keep.tile([P, N], U32, name="we_codes", align_bytes=64)
+        we_scales = keep.tile([P, N], U8, name="we_scales", align_bytes=64)
+        wgo_sb = keep.tile([P, S], F32, name="wgo_sb")
+        gmax_sb = keep.tile([P, PACK], F32, name="gmax_sb")
+        gmax_turn = keep.tile([P, PACK], F32, name="gmax_turn")
+        gwave_sb = keep.tile([P, PACK], F32, name="gwave_sb")
+        ident = keep.tile([P, P], F32, name="ident")
+        minus_anchor = keep.tile([P, P], F32, name="minus_anchor")
+        pages = [keep.tile([P, T2], F32, name="page%d" % b) for b in range(ROW_BLOCKS)]
+
+        def load_table(a):
+            nc.sync.dma_start(table[a][:], tab_words[a].rearrange("p t i -> p (t i)").bitcast(I32))
+
+        def load_rows(rows):
+            raw = stage.tile([P, PACK, rows.shape[1]], F32, name="raw", tag="raw", bufs=3)
+            nc.sync.dma_start(raw[:], rows.rearrange("(p j) w -> p j w", j=PACK))
+            return raw
+
+        def quantise_rows(raw, codes, scales, on_gpsimd=False):
+            width = raw.shape[2]
+            grouped = stage.tile([P, width, PACK], BF16, name="grouped", tag="grouped", bufs=3, align_bytes=64)
+            if on_gpsimd:
+                nc.gpsimd.tensor_scalar(grouped[:], raw[:].rearrange("p t c -> p c t"), 1.0, 0.0, ALU.mult, ALU.add)
+            else:
+                nc.scalar.copy(
+                    grouped[:].rearrange("p (c i) t -> p c t i", i=4),
+                    raw[:].rearrange("p t (c i) -> p c t i", i=4),
+                )
+            nc.vector.quantize_mx(codes.bitcast(FP8X4), scales, grouped[:].rearrange("p w j -> p (w j)"))
+
+        picked = {}
+
+        def gather_words(c, a):
+            if a == 0:
+                scales = work.tile([P, CHUNK], U8, name="scales_a", bufs=GATHER_AHEAD, align_bytes=64)
+                nc.vector.tensor_copy(
+                    scales[:], table_scales[:].indirect(list_a[:, c * CHUNK // 16 : (c + 1) * CHUNK // 16])
+                )
+                picked["scales", c] = scales
+            for side, offsets in (("a", list_a), ("b", list_b)):
+                words = work.tile([P, CHUNK], U32, name="words_%s%d" % (side, a), bufs=GATHER_AHEAD, align_bytes=64)
+                nc.vector.tensor_copy(
+                    words[:], table[a][:].bitcast(U32).indirect(offsets[:, c * CHUNK // 16 : (c + 1) * CHUNK // 16])
+                )
+                picked[side, a, c] = words
+
+        nc.gpsimd.memset(table_scales[:].bitcast(I32), 0)
+        nc.sync.dma_start(list_b[:], offs2)
+        nc.sync.dma_start(list_a[:], offs)
+        load_table(0)
+        for q in range(4):
+            nc.sync.dma_start(
+                table_scales[32 * q : 32 * q + 4 * PASSES, :].bitcast(I32),
+                tab_scales[:, 4 * q : 4 * q + 4, :].bitcast(I32),
+            )
+        wa_raw = [load_rows(wa[0:512, :])]
+        nc.gpsimd.memset(wb_scales_sb[:].rearrange("p a c -> p (a c)").bitcast(I32), 0)
+        nc.gpsimd.memset(wc_scales_sb[:].bitcast(I32), 0)
+        for a in range(1, PASSES):
+            nc.gpsimd.memset(v2_scales[a][:].bitcast(I32), 0)
+        for b in range(4):
+            nc.vector.memset(pages[b][:].bitcast(I32), 0)
+        nc.vector.tensor_copy(v2_scales[0][:], table_scales[:].indirect(list_b[:]))
+        for a in range(1, PASSES):
+            nc.sync.dma_start(
+                v2_scales[a][0 : P - 4 * a, :].bitcast(I32), v2_scales[0][4 * a : P, :].bitcast(I32)
+            )
+        wa_raw.append(load_rows(wa[512:1024, :]))
+        wa_raw.append(load_rows(wa[1024:1536, :]))
+        load_table(1)
+        for q in range(4):
+            nc.sync.dma_start(
+                wb_scales_sb[32 * q : 32 * q + 4, :, :].bitcast(I32),
+                wb_scales[:, 4 * q : 4 * q + 4, :].rearrange("a r c -> r a c").bitcast(I32),
+            )
+        load_table(2)
+        nc.sync.dma_start(wb_sb[:].bitcast(I32), wb_words.rearrange("a p c -> p a c").bitcast(I32))
+
+        make_identity(nc, ident[:])
+        nc.gpsimd.memset(minus_anchor[:], -ANCHOR)
+        for b in range(4, ROW_BLOCKS):
+            nc.gpsimd.memset(pages[b][:], 0.0)
+
+        for a in range(PASSES):
+            quantise_rows(wa_raw[a], wa_codes[a][:], wa_scales[a][:])
+            for c in range(GATHER_AHEAD):
+                gather_words(c, a)
+
+        nc.sync.dma_start(gmax_sb[:], gmax.rearrange("(p t) -> p t", t=PACK))
+        nc.sync.dma_start(gwave_sb[:], gwave.rearrange("(p t) -> p t", t=PACK))
+        we_raw = [load_rows(we[:, h * WE_HALF : (h + 1) * WE_HALF]) for h in range(2)]
+        nc.sync.dma_start(wc_sb[:].bitcast(I32), wc_words[0].bitcast(I32))
+        for q in range(4):
+            nc.sync.dma_start(
+                wc_scales_sb[32 * q : 32 * q + 4, :].bitcast(I32),
+                wc_scales[0, 4 * q : 4 * q + 4, :].bitcast(I32),
+            )
+        nc.sync.dma_start(list_out[:], offs3)
+        nc.sync.dma_start(wgo_sb[:], wgo)
+        nc.vector.tensor_scalar(gmax_turn[:], gmax_sb[:], TURN, None, ALU.mult)
+
+        state = {}
+
+        def project(i):
+            cols = slice(i * BLOCK, (i + 1) * BLOCK)
+            c, half = divmod(i, 2)
+            part = slice(half * BLOCK, (half + 1) * BLOCK)
+            a_ps = psum.tile([P, H], F32, name="a_ps", tag="proj", bufs=3)
+            for a in range(PASSES):
+                nc.tensor.matmul_mx(
+                    a_ps[:], lhsT=picked["a", a, c][:, part].bitcast(FP8X4), lhsT_scale=picked["scales", c][4 * a : P, part],
+                    rhs=wa_codes[a][:].bitcast(FP8X4), rhs_scale=wa_scales[a][:],
+                    start=(a == 0), stop=(a == PASSES - 1),
+                )
+            b_ps = psum.tile([P, H], F32, name="b_ps", tag="proj", bufs=3)
+            for a in range(PASSES):
+                nc.tensor.matmul_mx(
+                    b_ps[:], lhsT=picked["b", a, c][:, part].bitcast(FP8X4), lhsT_scale=v2_scales[a][:, cols],
+                    rhs=wb_sb[:, a, :].bitcast(FP4X4), rhs_scale=wb_scales_sb[:, a, :],
+                    start=(a == 0), stop=(a == PASSES - 1),
+                )
+            turns = work.tile([P, 2, PACK, P], F32, name="turns", bufs=3)
+            nc.scalar.activation(turns[:, 0], a_ps[:].rearrange("p (m t) -> p t m", t=PACK), ACT.Copy, scale=1.0 / TURN)
+            nc.scalar.activation(
+                turns[:, 1], b_ps[:].rearrange("p (m t) -> p t m", t=PACK), ACT.Copy, scale=1.0 / TURN, bias=0.25
+            )
+            whole = work.tile([P, 2, PACK, P], U32, name="whole")
+            nc.scalar.activation(
+                whole[:].rearrange("p s t m -> p (s t m)"), turns[:].rearrange("p s t m -> p (s t m)"),
+                ACT.Copy, scale=-ULPS_PER_TURN, bias=ANCHOR_BITS,
+            )
+            larger = work.tile([P, PACK, P], F32, name="larger", bufs=2)
+            nc.vector.scalar_tensor_tensor(larger[:], turns[:, 1], -0.25, turns[:, 0], ALU.add, ALU.max)
+            state[i] = (turns, whole, larger)
+
+        def waves(i):
+            turns, whole, larger = state[i]
+            c, half = divmod(i, 2)
+            if half == 0:
+                trig = work.tile([P, 2, PACK, CHUNK], F32, name="trig")
+                z1 = work.tile([P, PACK, CHUNK], BF16, name="z1")
+                state["chunk", c] = (trig, z1)
+            trig, z1 = state["chunk", c]
+            cols = slice(half * BLOCK, (half + 1) * BLOCK)
+            for s in range(2):
+                reduced = psum.tile([P, PACK, BLOCK], F32, name="reduced", tag="reduced", bufs=4)
+                for t in range(PACK):
+                    terms = (whole[:, s, t, :].bitcast(F32), minus_anchor[:], turns[:, s, t, :])
+                    for n, term in enumerate(terms):
+                        nc.tensor.matmul(
+                            reduced[:, t, :], lhsT=term, rhs=ident[:], is_transpose=True,
+                            start=(n == 0), stop=(n == len(terms) - 1),
+                        )
+                nc.scalar.activation(trig[:, s, :, cols], reduced[:], ACT.Sin, scale=TURN)
+
+        def scale_larger(i):
+            turns, whole, larger = state[i]
+            c, half = divmod(i, 2)
+            trig, z1 = state["chunk", c]
+            cols = slice(half * BLOCK, (half + 1) * BLOCK)
+            larger_ps = psum.tile([P, PACK, BLOCK], F32, name="larger_ps", tag="ly", bufs=1)
+            for t in range(PACK):
+                nc.tensor.transpose(larger_ps[:, t, :], larger[:, t, :], ident[:])
+            for t in range(PACK):
+                nc.scalar.activation(z1[:, t, cols], larger_ps[:, t, :], ACT.Copy, scale=gmax_turn[:, t : t + 1])
+
+        def features(c):
+            trig, z1 = state["chunk", c]
+            z2 = work.tile([P, PACK, CHUNK], BF16, name="z2")
+            for t in range(PACK):
+                nc.vector.scalar_tensor_tensor(
+                    z2[:, t, :], trig[:, 0, t, :], gwave_sb[:, t : t + 1], trig[:, 1, t, :], ALU.mult, ALU.mult
+                )
+            z1_grouped = work.tile([P, CHUNK, PACK], BF16, name="z1_grouped", align_bytes=64)
+            z2_grouped = work.tile([P, CHUNK, PACK], BF16, name="z2_grouped", align_bytes=64)
+            nc.scalar.copy(
+                z1_grouped[:].rearrange("p (c i) t -> p c t i", i=4), z1[:].rearrange("p t (c i) -> p c t i", i=4)
+            )
+            nc.vector.tensor_copy(
+                z2_grouped[:].rearrange("p (c i) t -> p c t i", i=4), z2[:].rearrange("p t (c i) -> p c t i", i=4)
+            )
+            z_codes = work.tile([P, 2, CHUNK], U32, name="z_codes", align_bytes=64)
+            z_scales = work.tile([P, 2, CHUNK], U8, name="z_scales", align_bytes=64)
+            for s, grouped in enumerate((z1_grouped, z2_grouped)):
+                nc.vector.quantize_mx(
+                    z_codes[:, s, :].bitcast(FP8X4), z_scales[:, s, :], grouped[:].rearrange("p w j -> p (w j)")
+                )
+            state["z", c] = (z_codes, z_scales)
+
+        def place(c, pair):
+            z_codes, z_scales = state["z", c]
+            if True:
+                y_ps = psum.tile([P, 2, CHUNK], F32, name="y_ps", tag="ly", bufs=1)
+                for u in range(2):
+                    b = 2 * pair + u
+                    rows = slice(b * P, (b + 1) * P)
+                    nc.tensor.matmul_mx(
+                        y_ps[:, u, :], lhsT=wc_sb[:, 2 * b * P : 2 * (b + 1) * P].bitcast(FP4X4),
+                        lhsT_scale=wc_scales_sb[:, rows], rhs=z_codes[:, 0, :].bitcast(FP8X4),
+                        rhs_scale=z_scales[:, 0, :], start=True, stop=False,
+                    )
+                    nc.tensor.matmul_mx(
+                        y_ps[:, u, :], lhsT=we_codes[:, rows].bitcast(FP8X4), lhsT_scale=we_scales[:, rows],
+                        rhs=z_codes[:, 1, :].bitcast(FP8X4), rhs_scale=z_scales[:, 1, :], start=False, stop=True,
+                    )
+                y = work.tile([P, 2, CHUNK], F32, name="y", bufs=4)
+                nc.scalar.activation(y[:], y_ps[:], ACT.Tanh)
+                for u in range(2):
+                    b = 2 * pair + u
+                    nc.vector.tensor_tensor(
+                        pages[b][:].indirect(list_out[:, c * CHUNK // 16 : (c + 1) * CHUNK // 16]),
+                        y[:, u, :], wgo_sb[:, c * CHUNK : (c + 1) * CHUNK], ALU.mult,
+                    )
+                    if c == CHUNKS - 1:
+                        nc.sync.dma_start(out[b * P : (b + 1) * P, :], pages[b][:])
+
+        def later_gathers(c):
+            if c + GATHER_AHEAD < CHUNKS:
+                for a in range(PASSES):
+                    gather_words(c + GATHER_AHEAD, a)
+
+        def quantise_we():
+            for h in range(2):
+                cols = slice(h * WE_HALF, (h + 1) * WE_HALF)
+                quantise_rows(we_raw[h], we_codes[:, cols], we_scales[:, cols], True)
+
+        project(0)
+        for c in range(CHUNKS):
+            project(2 * c + 1)
+            later_gathers(c)
+            if c > 0:
+                place(c - 1, 1)
+            waves(2 * c)
+            scale_larger(2 * c)
+            waves(2 * c + 1)
+            scale_larger(2 * c + 1)
+            if c == 0:
+                quantise_we()
+            features(c)
+            if c > 0:
+                place(c - 1, 2)
+            if c + 1 < CHUNKS:
+                project(2 * c + 2)
+            place(c, 0)
+        place(CHUNKS - 1, 1)
+        place(CHUNKS - 1, 2)

@@ -26,6 +26,7 @@ CHUNK = 256
 ROW_BLOCKS = N // P
 WE_HALF = N // 2
 CHUNKS = S // CHUNK
+AHEAD = (4, 2, 2)
 GATHER_AHEAD = 2
 TURN = 2.0 * math.pi
 ANCHOR = 98304.0
@@ -47,7 +48,7 @@ def tile_list_mesh_link_features_kernel(
         list_a = keep.tile([P, S // 16], U16, name="list_a")
         list_b = keep.tile([P, S // 16], U16, name="list_b")
         list_out = keep.tile([P, S // 16], U16, name="list_out")
-        table = [keep.tile([P, T], I32, name="table%d" % a, align_bytes=64) for a in range(PASSES)]
+        table = [keep.tile([P, T], I32, name="table%d" % a, tag="table", bufs=PASSES, align_bytes=64) for a in range(PASSES)]
         table_scales = keep.tile([P, T], U8, name="table_scales", align_bytes=64)
         v2_scales = [keep.tile([P, S], U8, name="v2_scales%d" % a, align_bytes=64) for a in range(PASSES)]
         wa_codes = [keep.tile([P, H], U32, name="wa_codes%d" % a, align_bytes=64) for a in range(PASSES)]
@@ -64,44 +65,44 @@ def tile_list_mesh_link_features_kernel(
         gwave_sb = keep.tile([P, PACK], F32, name="gwave_sb")
         ident = keep.tile([P, P], F32, name="ident")
         minus_anchor = keep.tile([P, P], F32, name="minus_anchor")
-        pages = [keep.tile([P, T2], F32, name="page%d" % b) for b in range(ROW_BLOCKS)]
+        pages = [keep.tile([P, T2], F32, name="page%d" % b) for b in range(3)]
 
         def load_table(a):
             nc.sync.dma_start(table[a][:], tab_words[a].rearrange("p t i -> p (t i)").bitcast(I32))
 
         def load_rows(rows):
-            raw = stage.tile([P, PACK, rows.shape[1]], F32, name="raw", tag="raw", bufs=3)
+            raw = stage.tile([P, PACK, rows.shape[1]], F32, name="raw", tag="raw", bufs=4)
             nc.sync.dma_start(raw[:], rows.rearrange("(p j) w -> p j w", j=PACK))
             return raw
 
-        def quantise_rows(raw, codes, scales, on_gpsimd=False):
+        def quantise_rows(raw, codes, scales):
             width = raw.shape[2]
             grouped = stage.tile([P, width, PACK], BF16, name="grouped", tag="grouped", bufs=3, align_bytes=64)
-            if on_gpsimd:
-                nc.gpsimd.tensor_scalar(grouped[:], raw[:].rearrange("p t c -> p c t"), 1.0, 0.0, ALU.mult, ALU.add)
-            else:
-                nc.scalar.copy(
-                    grouped[:].rearrange("p (c i) t -> p c t i", i=4),
-                    raw[:].rearrange("p t (c i) -> p c t i", i=4),
-                )
+            nc.scalar.copy(
+                grouped[:].rearrange("p (c i) t -> p c t i", i=4),
+                raw[:].rearrange("p t (c i) -> p c t i", i=4),
+            )
             nc.vector.quantize_mx(codes.bitcast(FP8X4), scales, grouped[:].rearrange("p w j -> p (w j)"))
 
         picked = {}
 
         def gather_words(c, a):
-            if a == 0:
-                scales = work.tile([P, CHUNK], U8, name="scales_a", bufs=GATHER_AHEAD, align_bytes=64)
+            if a == 1:
+                scales = work.tile([P, CHUNK], U8, name="scales_a", bufs=AHEAD[1], align_bytes=64)
                 nc.vector.tensor_copy(
                     scales[:], table_scales[:].indirect(list_a[:, c * CHUNK // 16 : (c + 1) * CHUNK // 16])
                 )
                 picked["scales", c] = scales
             for side, offsets in (("a", list_a), ("b", list_b)):
-                words = work.tile([P, CHUNK], U32, name="words_%s%d" % (side, a), bufs=GATHER_AHEAD, align_bytes=64)
+                words = work.tile([P, CHUNK], U32, name="words_%s%d" % (side, a), bufs=AHEAD[a], align_bytes=64)
                 nc.vector.tensor_copy(
                     words[:], table[a][:].bitcast(U32).indirect(offsets[:, c * CHUNK // 16 : (c + 1) * CHUNK // 16])
                 )
                 picked[side, a, c] = words
 
+        warm = keep.tile([P, 2], F32, name="warm")
+        nc.vector.memset(warm[:, 0:1], 0.0)
+        nc.scalar.activation(warm[:, 1:2], warm[:, 0:1], ACT.Silu)
         nc.gpsimd.memset(table_scales[:].bitcast(I32), 0)
         nc.sync.dma_start(list_b[:], offs2)
         nc.sync.dma_start(list_a[:], offs)
@@ -112,15 +113,15 @@ def tile_list_mesh_link_features_kernel(
                 tab_scales[:, 4 * q : 4 * q + 4, :].bitcast(I32),
             )
         wa_raw = [load_rows(wa[0:512, :])]
-        nc.gpsimd.memset(wb_scales_sb[:].rearrange("p a c -> p (a c)").bitcast(I32), 0)
-        nc.gpsimd.memset(wc_scales_sb[:].bitcast(I32), 0)
+        nc.vector.memset(wb_scales_sb[:].rearrange("p a c -> p (a c)").bitcast(I32), 0)
+        nc.vector.memset(wc_scales_sb[:].bitcast(I32), 0)
         for a in range(1, PASSES):
-            nc.gpsimd.memset(v2_scales[a][:].bitcast(I32), 0)
-        for b in range(4):
+            nc.vector.memset(v2_scales[a][:].bitcast(I32), 0)
+        for b in range(3):
             nc.vector.memset(pages[b][:].bitcast(I32), 0)
         nc.vector.tensor_copy(v2_scales[0][:], table_scales[:].indirect(list_b[:]))
         for a in range(1, PASSES):
-            nc.sync.dma_start(
+            nc.gpsimd.dma_start(
                 v2_scales[a][0 : P - 4 * a, :].bitcast(I32), v2_scales[0][4 * a : P, :].bitcast(I32)
             )
         wa_raw.append(load_rows(wa[512:1024, :]))
@@ -131,22 +132,21 @@ def tile_list_mesh_link_features_kernel(
                 wb_scales_sb[32 * q : 32 * q + 4, :, :].bitcast(I32),
                 wb_scales[:, 4 * q : 4 * q + 4, :].rearrange("a r c -> r a c").bitcast(I32),
             )
+        we_raw = [load_rows(we[:, 0:WE_HALF])]
         load_table(2)
         nc.sync.dma_start(wb_sb[:].bitcast(I32), wb_words.rearrange("a p c -> p a c").bitcast(I32))
 
         make_identity(nc, ident[:])
-        nc.gpsimd.memset(minus_anchor[:], -ANCHOR)
-        for b in range(4, ROW_BLOCKS):
-            nc.gpsimd.memset(pages[b][:], 0.0)
+        nc.vector.memset(minus_anchor[:], -ANCHOR)
 
         for a in range(PASSES):
             quantise_rows(wa_raw[a], wa_codes[a][:], wa_scales[a][:])
-            for c in range(GATHER_AHEAD):
+            for c in range(AHEAD[a]):
                 gather_words(c, a)
 
         nc.sync.dma_start(gmax_sb[:], gmax.rearrange("(p t) -> p t", t=PACK))
         nc.sync.dma_start(gwave_sb[:], gwave.rearrange("(p t) -> p t", t=PACK))
-        we_raw = [load_rows(we[:, h * WE_HALF : (h + 1) * WE_HALF]) for h in range(2)]
+        we_raw.append(load_rows(we[:, WE_HALF:N]))
         nc.sync.dma_start(wc_sb[:].bitcast(I32), wc_words[0].bitcast(I32))
         for q in range(4):
             nc.sync.dma_start(
@@ -273,32 +273,39 @@ def tile_list_mesh_link_features_kernel(
                         nc.sync.dma_start(out[b * P : (b + 1) * P, :], pages[b][:])
 
         def later_gathers(c):
-            if c + GATHER_AHEAD < CHUNKS:
-                for a in range(PASSES):
-                    gather_words(c + GATHER_AHEAD, a)
+            for a in range(PASSES):
+                if c + AHEAD[a] < CHUNKS:
+                    gather_words(c + AHEAD[a], a)
 
-        def quantise_we():
-            for h in range(2):
-                cols = slice(h * WE_HALF, (h + 1) * WE_HALF)
-                quantise_rows(we_raw[h], we_codes[:, cols], we_scales[:, cols], True)
+        def late_pages():
+            for b in range(PASSES, ROW_BLOCKS):
+                pages.append(keep.tile([P, T2], F32, name="late_page", tag="table", bufs=PASSES, align_bytes=64))
+                nc.gpsimd.memset(pages[b][:], 0.0)
 
+        def quantise_we(h):
+            cols = slice(h * WE_HALF, (h + 1) * WE_HALF)
+            quantise_rows(we_raw[h], we_codes[:, cols], we_scales[:, cols])
+
+        quantise_we(0)
         project(0)
         for c in range(CHUNKS):
             project(2 * c + 1)
             later_gathers(c)
+            if c == CHUNKS - 1 - min(AHEAD):
+                late_pages()
             if c > 0:
                 place(c - 1, 1)
             waves(2 * c)
             scale_larger(2 * c)
             waves(2 * c + 1)
             scale_larger(2 * c + 1)
-            if c == 0:
-                quantise_we()
             features(c)
             if c > 0:
                 place(c - 1, 2)
             if c + 1 < CHUNKS:
                 project(2 * c + 2)
             place(c, 0)
+            if c == 0:
+                quantise_we(1)
         place(CHUNKS - 1, 1)
         place(CHUNKS - 1, 2)

@@ -20,18 +20,25 @@ ALU = mybir.AluOpType
 
 P = 128
 PACK = 4
-PASSES = K // (P * PACK)
+K_PASS = P * PACK
+PASSES = K // K_PASS
+QUADRANTS = 4
+PER_COLUMN = 16
 BLOCK = 128
 CHUNK = 256
-ROW_BLOCKS = N // P
-WE_HALF = N // 2
 CHUNKS = S // CHUNK
-AHEAD = (4, 2, 2)
-GATHER_AHEAD = 2
+LAST = CHUNKS - 1
+ROW_BLOCKS = N // P
+PAIRS = ROW_BLOCKS // 2
+WE_HALF = N // 2
+EARLY_PAGES = 3
 TURN = 2.0 * math.pi
+QUARTER = 0.25
 ANCHOR = 98304.0
 ANCHOR_BITS = 1203765248.0
 ULPS_PER_TURN = 128.0
+EARLY = [[(0, 1), (2, 3)], [(0, 1)], [(0,), (1,)]]
+LATE = [[], [(), (2, 3)][1:], [(2, 3)]]
 
 
 def tile_list_mesh_link_features_kernel(
@@ -41,18 +48,18 @@ def tile_list_mesh_link_features_kernel(
     nc = tc.nc
     with ExitStack() as ctx:
         keep = ctx.enter_context(tc.tile_pool(name="keep", bufs=1))
-        stage = ctx.enter_context(tc.tile_pool(name="stage", bufs=2))
+        stage = ctx.enter_context(tc.tile_pool(name="stage", bufs=3))
         work = ctx.enter_context(tc.tile_pool(name="work", bufs=2))
         psum = ctx.enter_context(tc.psum_pool(name="psum", bufs=1))
 
-        list_a = keep.tile([P, S // 16], U16, name="list_a")
-        list_b = keep.tile([P, S // 16], U16, name="list_b")
-        list_out = keep.tile([P, S // 16], U16, name="list_out")
-        table = [keep.tile([P, T], I32, name="table%d" % a, tag="table", bufs=PASSES, align_bytes=64) for a in range(PASSES)]
+        list_a = keep.tile([P, S // PER_COLUMN], U16, name="list_a")
+        list_b = keep.tile([P, S // PER_COLUMN], U16, name="list_b")
+        list_out = keep.tile([P, S // PER_COLUMN], U16, name="list_out")
+        table = [keep.tile([P, T], I32, name="table%d" % g, align_bytes=64) for g in range(PASSES)]
         table_scales = keep.tile([P, T], U8, name="table_scales", align_bytes=64)
-        v2_scales = [keep.tile([P, S], U8, name="v2_scales%d" % a, align_bytes=64) for a in range(PASSES)]
-        wa_codes = [keep.tile([P, H], U32, name="wa_codes%d" % a, align_bytes=64) for a in range(PASSES)]
-        wa_scales = [keep.tile([P, H], U8, name="wa_scales%d" % a, align_bytes=64) for a in range(PASSES)]
+        scales_b = [keep.tile([P, S], U8, name="scales_b%d" % g, align_bytes=64) for g in range(PASSES)]
+        wa_codes = [keep.tile([P, H], U32, name="wa_codes%d" % g, align_bytes=64) for g in range(PASSES)]
+        wa_scales = [keep.tile([P, H], U8, name="wa_scales%d" % g, align_bytes=64) for g in range(PASSES)]
         wb_sb = keep.tile([P, PASSES, 2 * H], U8, name="wb_sb", align_bytes=64)
         wb_scales_sb = keep.tile([P, PASSES, H], U8, name="wb_scales_sb", align_bytes=64)
         wc_sb = keep.tile([P, 2 * N], U8, name="wc_sb", align_bytes=64)
@@ -65,90 +72,110 @@ def tile_list_mesh_link_features_kernel(
         gwave_sb = keep.tile([P, PACK], F32, name="gwave_sb")
         ident = keep.tile([P, P], F32, name="ident")
         minus_anchor = keep.tile([P, P], F32, name="minus_anchor")
-        pages = [keep.tile([P, T2], F32, name="page%d" % b) for b in range(3)]
+        warm = keep.tile([P, 2], F32, name="warm")
+        y_wide = keep.tile([P, 2, 2, CHUNK], F32, name="y_wide")
+        pages = [keep.tile([P, T2], F32, name="page%d" % b) for b in range(EARLY_PAGES)]
+        picked, angles, waves, operands = {}, {}, {}, {}
 
-        def load_table(a):
-            nc.sync.dma_start(table[a][:], tab_words[a].rearrange("p t i -> p (t i)").bitcast(I32))
+        def load_table(g):
+            nc.sync.dma_start(table[g][:], tab_words[g].rearrange("p t i -> p (t i)").bitcast(I32))
 
         def load_rows(rows):
-            raw = stage.tile([P, PACK, rows.shape[1]], F32, name="raw", tag="raw", bufs=4)
-            nc.sync.dma_start(raw[:], rows.rearrange("(p j) w -> p j w", j=PACK))
+            raw = stage.tile([P, PACK, rows.shape[1]], F32, name="raw", bufs=4)
+            nc.sync.dma_start(raw[:], rows.rearrange("(p t) w -> p t w", t=PACK))
             return raw
 
-        def quantise_rows(raw, codes, scales):
-            width = raw.shape[2]
-            grouped = stage.tile([P, width, PACK], BF16, name="grouped", tag="grouped", bufs=3, align_bytes=64)
-            nc.scalar.copy(
+        def interleave(copy, grouped, slices):
+            copy(
                 grouped[:].rearrange("p (c i) t -> p c t i", i=4),
-                raw[:].rearrange("p t (c i) -> p c t i", i=4),
+                slices[:].rearrange("p t (c i) -> p c t i", i=4),
             )
-            nc.vector.quantize_mx(codes.bitcast(FP8X4), scales, grouped[:].rearrange("p w j -> p (w j)"))
 
-        picked = {}
+        def quantise(codes, scales, grouped):
+            nc.vector.quantize_mx(codes.bitcast(FP8X4), scales, grouped[:].rearrange("p w t -> p (w t)"))
 
-        def gather_words(c, a):
-            if a == 1:
-                scales = work.tile([P, CHUNK], U8, name="scales_a", bufs=AHEAD[1], align_bytes=64)
-                nc.vector.tensor_copy(
-                    scales[:], table_scales[:].indirect(list_a[:, c * CHUNK // 16 : (c + 1) * CHUNK // 16])
-                )
-                picked["scales", c] = scales
-            for side, offsets in (("a", list_a), ("b", list_b)):
-                words = work.tile([P, CHUNK], U32, name="words_%s%d" % (side, a), bufs=AHEAD[a], align_bytes=64)
-                nc.vector.tensor_copy(
-                    words[:], table[a][:].bitcast(U32).indirect(offsets[:, c * CHUNK // 16 : (c + 1) * CHUNK // 16])
-                )
-                picked[side, a, c] = words
+        def quantise_rows(raw, codes, scales, copy=nc.scalar.copy):
+            grouped = stage.tile([P, raw.shape[2], PACK], BF16, name="grouped", align_bytes=64)
+            interleave(copy, grouped, raw)
+            quantise(codes, scales, grouped)
 
-        warm = keep.tile([P, 2], F32, name="warm")
+        def quantise_we(half):
+            cols = slice(half * WE_HALF, (half + 1) * WE_HALF)
+            quantise_rows(we_raw[half], we_codes[:, cols], we_scales[:, cols], nc.vector.tensor_copy if half in (0,) else nc.scalar.copy)
+
+        def entries(offsets, lo, hi):
+            return offsets[:, lo // PER_COLUMN : hi // PER_COLUMN]
+
+        def gather(name, window, offsets, dtype, chunks, bufs):
+            lo, hi = chunks[0] * CHUNK, (chunks[-1] + 1) * CHUNK
+            dst = work.tile([P, hi - lo], dtype, name=name, bufs=bufs, align_bytes=64)
+            nc.vector.tensor_copy(dst[:], window.indirect(entries(offsets, lo, hi)))
+            for c in chunks:
+                picked[name, c] = dst[:, c * CHUNK - lo : (c + 1) * CHUNK - lo]
+
+        def gather_pass(g, pieces):
+            for chunks in pieces:
+                if g == 1:
+                    gather("scales_a", table_scales[:], list_a, U8, chunks, len(EARLY[g]))
+                for side, offsets in (("a", list_a), ("b", list_b)):
+                    gather("words_%s%d" % (side, g), table[g][:].bitcast(U32), offsets, U32, chunks, len(EARLY[g]))
+
+        def first_or_ring(c, shape, dtype, name, bufs=2):
+            if c == 0:
+                return keep.tile(shape, dtype, name=name + "_first", align_bytes=64)
+            return work.tile(shape, dtype, name=name, bufs=bufs, align_bytes=64)
+
+        def late_page(tenant):
+            page = keep.tile([P, T2], F32, name="late_page", tag=tenant + "_first", align_bytes=64)
+            nc.gpsimd.memset(page[:], 0.0)
+            pages.append(page)
+
         nc.vector.memset(warm[:, 0:1], 0.0)
         nc.scalar.activation(warm[:, 1:2], warm[:, 0:1], ACT.Silu)
+
         nc.gpsimd.memset(table_scales[:].bitcast(I32), 0)
         nc.sync.dma_start(list_b[:], offs2)
         nc.sync.dma_start(list_a[:], offs)
         load_table(0)
-        for q in range(4):
+        for q in range(QUADRANTS):
             nc.sync.dma_start(
                 table_scales[32 * q : 32 * q + 4 * PASSES, :].bitcast(I32),
                 tab_scales[:, 4 * q : 4 * q + 4, :].bitcast(I32),
             )
-        wa_raw = [load_rows(wa[0:512, :])]
-        nc.vector.memset(wb_scales_sb[:].rearrange("p a c -> p (a c)").bitcast(I32), 0)
+        wa_raw = [load_rows(wa[0:K_PASS, :])]
+        nc.vector.memset(wb_scales_sb[:].rearrange("p g c -> p (g c)").bitcast(I32), 0)
         nc.vector.memset(wc_scales_sb[:].bitcast(I32), 0)
-        for a in range(1, PASSES):
-            nc.vector.memset(v2_scales[a][:].bitcast(I32), 0)
-        for b in range(3):
-            nc.vector.memset(pages[b][:].bitcast(I32), 0)
-        nc.vector.tensor_copy(v2_scales[0][:], table_scales[:].indirect(list_b[:]))
-        for a in range(1, PASSES):
-            nc.gpsimd.dma_start(
-                v2_scales[a][0 : P - 4 * a, :].bitcast(I32), v2_scales[0][4 * a : P, :].bitcast(I32)
-            )
-        wa_raw.append(load_rows(wa[512:1024, :]))
-        wa_raw.append(load_rows(wa[1024:1536, :]))
+        for g in range(1, PASSES):
+            nc.vector.memset(scales_b[g][:].bitcast(I32), 0)
+        for page in pages:
+            nc.vector.memset(page[:].bitcast(I32), 0)
+        gather_pass(0, EARLY[0][:1])
+        nc.vector.tensor_copy(scales_b[0][:], table_scales[:].indirect(list_b[:]))
+        for g in range(1, PASSES):
+            nc.gpsimd.dma_start(scales_b[g][0 : P - 4 * g, :].bitcast(I32), scales_b[0][4 * g : P, :].bitcast(I32))
+        wa_raw.append(load_rows(wa[K_PASS : 2 * K_PASS, :]))
         load_table(1)
-        for q in range(4):
+        wa_raw.append(load_rows(wa[2 * K_PASS : K, :]))
+        for q in range(QUADRANTS):
             nc.sync.dma_start(
                 wb_scales_sb[32 * q : 32 * q + 4, :, :].bitcast(I32),
-                wb_scales[:, 4 * q : 4 * q + 4, :].rearrange("a r c -> r a c").bitcast(I32),
+                wb_scales[:, 4 * q : 4 * q + 4, :].rearrange("g r c -> r g c").bitcast(I32),
             )
-        we_raw = [load_rows(we[:, 0:WE_HALF])]
         load_table(2)
-        nc.sync.dma_start(wb_sb[:].bitcast(I32), wb_words.rearrange("a p c -> p a c").bitcast(I32))
-
+        nc.sync.dma_start(wb_sb[:].bitcast(I32), wb_words.rearrange("g p c -> p g c").bitcast(I32))
+        we_raw = [load_rows(we[:, 0:WE_HALF])]
         make_identity(nc, ident[:])
         nc.vector.memset(minus_anchor[:], -ANCHOR)
 
-        for a in range(PASSES):
-            quantise_rows(wa_raw[a], wa_codes[a][:], wa_scales[a][:])
-            for c in range(AHEAD[a]):
-                gather_words(c, a)
+        for g in range(PASSES):
+            quantise_rows(wa_raw[g], wa_codes[g][:], wa_scales[g][:])
+            gather_pass(g, EARLY[g][1 if g == 0 else 0 :])
 
         nc.sync.dma_start(gmax_sb[:], gmax.rearrange("(p t) -> p t", t=PACK))
         nc.sync.dma_start(gwave_sb[:], gwave.rearrange("(p t) -> p t", t=PACK))
         we_raw.append(load_rows(we[:, WE_HALF:N]))
         nc.sync.dma_start(wc_sb[:].bitcast(I32), wc_words[0].bitcast(I32))
-        for q in range(4):
+        for q in range(QUADRANTS):
             nc.sync.dma_start(
                 wc_scales_sb[32 * q : 32 * q + 4, :].bitcast(I32),
                 wc_scales[0, 4 * q : 4 * q + 4, :].bitcast(I32),
@@ -157,51 +184,47 @@ def tile_list_mesh_link_features_kernel(
         nc.sync.dma_start(wgo_sb[:], wgo)
         nc.vector.tensor_scalar(gmax_turn[:], gmax_sb[:], TURN, None, ALU.mult)
 
-        state = {}
-
         def project(i):
-            cols = slice(i * BLOCK, (i + 1) * BLOCK)
             c, half = divmod(i, 2)
             part = slice(half * BLOCK, (half + 1) * BLOCK)
-            a_ps = psum.tile([P, H], F32, name="a_ps", tag="proj", bufs=3)
-            for a in range(PASSES):
+            cols = slice(i * BLOCK, (i + 1) * BLOCK)
+            a_ps = psum.tile([P, H], F32, name="a_ps", tag="projection", bufs=3)
+            for g in reversed(range(PASSES)):
                 nc.tensor.matmul_mx(
-                    a_ps[:], lhsT=picked["a", a, c][:, part].bitcast(FP8X4), lhsT_scale=picked["scales", c][4 * a : P, part],
-                    rhs=wa_codes[a][:].bitcast(FP8X4), rhs_scale=wa_scales[a][:],
-                    start=(a == 0), stop=(a == PASSES - 1),
+                    a_ps[:], lhsT=picked["words_a%d" % g, c][:, part].bitcast(FP8X4),
+                    lhsT_scale=picked["scales_a", c][4 * g : P, part],
+                    rhs=wa_codes[g][:].bitcast(FP8X4), rhs_scale=wa_scales[g][:],
+                    start=(g == PASSES - 1), stop=(g == 0),
                 )
-            b_ps = psum.tile([P, H], F32, name="b_ps", tag="proj", bufs=3)
-            for a in range(PASSES):
+            b_ps = psum.tile([P, H], F32, name="b_ps", tag="projection", bufs=3)
+            for g in reversed(range(PASSES)):
                 nc.tensor.matmul_mx(
-                    b_ps[:], lhsT=picked["b", a, c][:, part].bitcast(FP8X4), lhsT_scale=v2_scales[a][:, cols],
-                    rhs=wb_sb[:, a, :].bitcast(FP4X4), rhs_scale=wb_scales_sb[:, a, :],
-                    start=(a == 0), stop=(a == PASSES - 1),
+                    b_ps[:], lhsT=picked["words_b%d" % g, c][:, part].bitcast(FP8X4), lhsT_scale=scales_b[g][:, cols],
+                    rhs=wb_sb[:, g, :].bitcast(FP4X4), rhs_scale=wb_scales_sb[:, g, :],
+                    start=(g == PASSES - 1), stop=(g == 0),
                 )
-            turns = work.tile([P, 2, PACK, P], F32, name="turns", bufs=3)
-            nc.scalar.activation(turns[:, 0], a_ps[:].rearrange("p (m t) -> p t m", t=PACK), ACT.Copy, scale=1.0 / TURN)
-            nc.scalar.activation(
-                turns[:, 1], b_ps[:].rearrange("p (m t) -> p t m", t=PACK), ACT.Copy, scale=1.0 / TURN, bias=0.25
-            )
+            turns = work.tile([P, 2, PACK, P], F32, name="turns", bufs=2)
             whole = work.tile([P, 2, PACK, P], U32, name="whole")
-            nc.scalar.activation(
-                whole[:].rearrange("p s t m -> p (s t m)"), turns[:].rearrange("p s t m -> p (s t m)"),
-                ACT.Copy, scale=-ULPS_PER_TURN, bias=ANCHOR_BITS,
-            )
-            larger = work.tile([P, PACK, P], F32, name="larger", bufs=2)
-            nc.vector.scalar_tensor_tensor(larger[:], turns[:, 1], -0.25, turns[:, 0], ALU.add, ALU.max)
-            state[i] = (turns, whole, larger)
+            for s, (ps, shift) in enumerate(((a_ps, 0.0), (b_ps, QUARTER))):
+                nc.scalar.activation(
+                    turns[:, s], ps[:].rearrange("p (m t) -> p t m", t=PACK), ACT.Copy, scale=1.0 / TURN, bias=shift
+                )
+                nc.scalar.activation(whole[:, s], turns[:, s], ACT.Copy, scale=-ULPS_PER_TURN, bias=ANCHOR_BITS)
+            larger = work.tile([P, PACK, P], F32, name="larger")
+            nc.vector.scalar_tensor_tensor(larger[:], turns[:, 1], -QUARTER, turns[:, 0], ALU.add, ALU.max)
+            angles[i] = (turns, whole, larger)
 
-        def waves(i):
-            turns, whole, larger = state[i]
+        def sines(i):
+            turns, whole, larger = angles[i]
             c, half = divmod(i, 2)
             if half == 0:
-                trig = work.tile([P, 2, PACK, CHUNK], F32, name="trig")
-                z1 = work.tile([P, PACK, CHUNK], BF16, name="z1")
-                state["chunk", c] = (trig, z1)
-            trig, z1 = state["chunk", c]
-            cols = slice(half * BLOCK, (half + 1) * BLOCK)
+                waves[c] = (
+                    work.tile([P, 2, PACK, CHUNK], F32, name="trig"),
+                    work.tile([P, PACK, CHUNK], BF16, name="z1"),
+                )
+            trig = waves[c][0]
             for s in range(2):
-                reduced = psum.tile([P, PACK, BLOCK], F32, name="reduced", tag="reduced", bufs=4)
+                reduced = psum.tile([P, PACK, BLOCK], F32, name="reduced", bufs=4)
                 for t in range(PACK):
                     terms = (whole[:, s, t, :].bitcast(F32), minus_anchor[:], turns[:, s, t, :])
                     for n, term in enumerate(terms):
@@ -209,103 +232,96 @@ def tile_list_mesh_link_features_kernel(
                             reduced[:, t, :], lhsT=term, rhs=ident[:], is_transpose=True,
                             start=(n == 0), stop=(n == len(terms) - 1),
                         )
-                nc.scalar.activation(trig[:, s, :, cols], reduced[:], ACT.Sin, scale=TURN)
+                nc.scalar.activation(
+                    trig[:, s, :, half * BLOCK : (half + 1) * BLOCK], reduced[:], ACT.Sin, scale=TURN
+                )
 
         def scale_larger(i):
-            turns, whole, larger = state[i]
+            larger = angles[i][2]
             c, half = divmod(i, 2)
-            trig, z1 = state["chunk", c]
-            cols = slice(half * BLOCK, (half + 1) * BLOCK)
-            larger_ps = psum.tile([P, PACK, BLOCK], F32, name="larger_ps", tag="ly", bufs=1)
+            z1 = waves[c][1]
+            larger_ps = psum.tile([P, PACK, BLOCK], F32, name="larger_ps", tag="shared")
             for t in range(PACK):
                 nc.tensor.transpose(larger_ps[:, t, :], larger[:, t, :], ident[:])
             for t in range(PACK):
-                nc.scalar.activation(z1[:, t, cols], larger_ps[:, t, :], ACT.Copy, scale=gmax_turn[:, t : t + 1])
+                nc.scalar.activation(
+                    z1[:, t, half * BLOCK : (half + 1) * BLOCK], larger_ps[:, t, :], ACT.Copy,
+                    scale=gmax_turn[:, t : t + 1],
+                )
 
         def features(c):
-            trig, z1 = state["chunk", c]
+            trig, z1 = waves[c]
             z2 = work.tile([P, PACK, CHUNK], BF16, name="z2")
             for t in range(PACK):
                 nc.vector.scalar_tensor_tensor(
                     z2[:, t, :], trig[:, 0, t, :], gwave_sb[:, t : t + 1], trig[:, 1, t, :], ALU.mult, ALU.mult
                 )
-            z1_grouped = work.tile([P, CHUNK, PACK], BF16, name="z1_grouped", align_bytes=64)
-            z2_grouped = work.tile([P, CHUNK, PACK], BF16, name="z2_grouped", align_bytes=64)
-            nc.scalar.copy(
-                z1_grouped[:].rearrange("p (c i) t -> p c t i", i=4), z1[:].rearrange("p t (c i) -> p c t i", i=4)
-            )
-            nc.vector.tensor_copy(
-                z2_grouped[:].rearrange("p (c i) t -> p c t i", i=4), z2[:].rearrange("p t (c i) -> p c t i", i=4)
-            )
+            z1_grouped = first_or_ring(c, [P, CHUNK, PACK], BF16, "z1_grouped")
+            z2_grouped = first_or_ring(c, [P, CHUNK, PACK], BF16, "z2_grouped")
+            interleave(nc.scalar.copy, z1_grouped, z1)
+            interleave(nc.vector.tensor_copy, z2_grouped, z2)
             z_codes = work.tile([P, 2, CHUNK], U32, name="z_codes", align_bytes=64)
             z_scales = work.tile([P, 2, CHUNK], U8, name="z_scales", align_bytes=64)
             for s, grouped in enumerate((z1_grouped, z2_grouped)):
-                nc.vector.quantize_mx(
-                    z_codes[:, s, :].bitcast(FP8X4), z_scales[:, s, :], grouped[:].rearrange("p w j -> p (w j)")
+                quantise(z_codes[:, s, :], z_scales[:, s, :], grouped)
+            operands[c] = (z_codes, z_scales)
+            if c == 0:
+                late_page("z2_grouped")
+                late_page("z1_grouped")
+
+        def outputs(c, pair, y):
+            z_codes, z_scales = operands[c]
+            y_ps = psum.tile([P, 2, CHUNK], F32, name="y_ps", tag="shared")
+            for u in range(2):
+                b = 2 * pair + u
+                rows = slice(b * P, (b + 1) * P)
+                nc.tensor.matmul_mx(
+                    y_ps[:, u, :], lhsT=wc_sb[:, 2 * b * P : 2 * (b + 1) * P].bitcast(FP4X4),
+                    lhsT_scale=wc_scales_sb[:, rows], rhs=z_codes[:, 0, :].bitcast(FP8X4),
+                    rhs_scale=z_scales[:, 0, :], start=True, stop=False,
                 )
-            state["z", c] = (z_codes, z_scales)
+                nc.tensor.matmul_mx(
+                    y_ps[:, u, :], lhsT=we_codes[:, rows].bitcast(FP8X4), lhsT_scale=we_scales[:, rows],
+                    rhs=z_codes[:, 1, :].bitcast(FP8X4), rhs_scale=z_scales[:, 1, :], start=False, stop=True,
+                )
+            nc.scalar.activation(y, y_ps[:], ACT.Tanh)
+
+        def scatter(b, values, lo, hi):
+            nc.vector.tensor_tensor(pages[b][:].indirect(entries(list_out, lo, hi)), values, wgo_sb[:, lo:hi], ALU.mult)
+            if hi == S:
+                nc.sync.dma_start(out[b * P : (b + 1) * P, :], pages[b][:])
 
         def place(c, pair):
-            z_codes, z_scales = state["z", c]
-            if True:
-                y_ps = psum.tile([P, 2, CHUNK], F32, name="y_ps", tag="ly", bufs=1)
-                for u in range(2):
-                    b = 2 * pair + u
-                    rows = slice(b * P, (b + 1) * P)
-                    nc.tensor.matmul_mx(
-                        y_ps[:, u, :], lhsT=wc_sb[:, 2 * b * P : 2 * (b + 1) * P].bitcast(FP4X4),
-                        lhsT_scale=wc_scales_sb[:, rows], rhs=z_codes[:, 0, :].bitcast(FP8X4),
-                        rhs_scale=z_scales[:, 0, :], start=True, stop=False,
-                    )
-                    nc.tensor.matmul_mx(
-                        y_ps[:, u, :], lhsT=we_codes[:, rows].bitcast(FP8X4), lhsT_scale=we_scales[:, rows],
-                        rhs=z_codes[:, 1, :].bitcast(FP8X4), rhs_scale=z_scales[:, 1, :], start=False, stop=True,
-                    )
-                y = work.tile([P, 2, CHUNK], F32, name="y", bufs=4)
-                nc.scalar.activation(y[:], y_ps[:], ACT.Tanh)
-                for u in range(2):
-                    b = 2 * pair + u
-                    nc.vector.tensor_tensor(
-                        pages[b][:].indirect(list_out[:, c * CHUNK // 16 : (c + 1) * CHUNK // 16]),
-                        y[:, u, :], wgo_sb[:, c * CHUNK : (c + 1) * CHUNK], ALU.mult,
-                    )
-                    if c == CHUNKS - 1:
-                        nc.sync.dma_start(out[b * P : (b + 1) * P, :], pages[b][:])
+            y = first_or_ring(c + pair, [P, 2, CHUNK], F32, "y", bufs=3)
+            outputs(c, pair, y[:])
+            for u in range(2):
+                scatter(2 * pair + u, y[:, u, :], c * CHUNK, (c + 1) * CHUNK)
+            if c + pair == 0:
+                late_page("y")
 
-        def later_gathers(c):
-            for a in range(PASSES):
-                if c + AHEAD[a] < CHUNKS:
-                    gather_words(c + AHEAD[a], a)
-
-        def late_pages():
-            for b in range(PASSES, ROW_BLOCKS):
-                pages.append(keep.tile([P, T2], F32, name="late_page", tag="table", bufs=PASSES, align_bytes=64))
-                nc.gpsimd.memset(pages[b][:], 0.0)
-
-        def quantise_we(h):
-            cols = slice(h * WE_HALF, (h + 1) * WE_HALF)
-            quantise_rows(we_raw[h], we_codes[:, cols], we_scales[:, cols])
-
+        slots = [[[], [], [(0, 0)]], [[(0, 1)], [(0, 2)], [(1, 0)]], [[(1, 1)], [(1, 2)], []], [[(2, 0)], [(2, 1)], [(3, 0), (3, 1)]]]
         quantise_we(0)
         project(0)
         for c in range(CHUNKS):
             project(2 * c + 1)
-            later_gathers(c)
-            if c == CHUNKS - 1 - min(AHEAD):
-                late_pages()
-            if c > 0:
-                place(c - 1, 1)
-            waves(2 * c)
+            for g in range(PASSES):
+                gather_pass(g, LATE[g][c : c + 1])
+            for pair in slots[c][0]:
+                place(*pair)
+            sines(2 * c)
+            sines(2 * c + 1)
             scale_larger(2 * c)
-            waves(2 * c + 1)
             scale_larger(2 * c + 1)
             features(c)
-            if c > 0:
-                place(c - 1, 2)
-            if c + 1 < CHUNKS:
+            for pair in slots[c][1]:
+                place(*pair)
+            if c < LAST:
                 project(2 * c + 2)
-            place(c, 0)
+            for pair in slots[c][2]:
+                place(*pair)
             if c == 0:
                 quantise_we(1)
-        place(CHUNKS - 1, 1)
-        place(CHUNKS - 1, 2)
+        for d in range(2):
+            outputs(LAST - 1 + d, PAIRS - 1, y_wide[:, :, d, :])
+        for u in range(2):
+            scatter(2 * (PAIRS - 1) + u, y_wide[:, u].rearrange("p d j -> p (d j)"), (LAST - 1) * CHUNK, S)

@@ -22,23 +22,27 @@ P = 128
 PACK = 4
 K_PASS = P * PACK
 PASSES = K // K_PASS
-QUADRANTS = 4
+QUADRANT = 32
+QUADRANTS = P // QUADRANT
+SCALE_ROWS = 4
 PER_COLUMN = 16
 BLOCK = 128
-CHUNK = 256
+CHUNK = 2 * BLOCK
 CHUNKS = S // CHUNK
 LAST = CHUNKS - 1
-ROW_BLOCKS = N // P
-PAIRS = ROW_BLOCKS // 2
+PAGES = N // P
+PAIRS = PAGES // 2
+LAST_PAIR = PAIRS - 1
 WE_HALF = N // 2
 EARLY_PAGES = 3
+RUN = 4
+REDUCED_BANKS = 4
+
 TURN = 2.0 * math.pi
 QUARTER = 0.25
 ANCHOR = 98304.0
 ANCHOR_BITS = 1203765248.0
 ULPS_PER_TURN = 128.0
-EARLY = [[(0, 1), (2, 3)], [(0, 1)], [(0,), (1,)]]
-LATE = [[], [(), (2, 3)][1:], [(2, 3)]]
 
 
 def tile_list_mesh_link_features_kernel(
@@ -75,53 +79,52 @@ def tile_list_mesh_link_features_kernel(
         warm = keep.tile([P, 2], F32, name="warm")
         y_wide = keep.tile([P, 2, 2, CHUNK], F32, name="y_wide")
         pages = [keep.tile([P, T2], F32, name="page%d" % b) for b in range(EARLY_PAGES)]
-        picked, angles, waves, operands = {}, {}, {}, {}
+        picked, angles, trig_of, z1_of, z2_of, operands = {}, {}, {}, {}, {}, {}
 
         def load_table(g):
             nc.sync.dma_start(table[g][:], tab_words[g].rearrange("p t i -> p (t i)").bitcast(I32))
 
         def load_rows(rows):
-            raw = stage.tile([P, PACK, rows.shape[1]], F32, name="raw", bufs=4)
+            raw = stage.tile([P, PACK, rows.shape[1]], F32, name="raw")
             nc.sync.dma_start(raw[:], rows.rearrange("(p t) w -> p t w", t=PACK))
             return raw
 
         def interleave(copy, grouped, slices):
             copy(
-                grouped[:].rearrange("p (c i) t -> p c t i", i=4),
-                slices[:].rearrange("p t (c i) -> p c t i", i=4),
+                grouped[:].rearrange("p (c i) t -> p c t i", i=RUN),
+                slices[:].rearrange("p t (c i) -> p c t i", i=RUN),
             )
 
         def quantise(codes, scales, grouped):
             nc.vector.quantize_mx(codes.bitcast(FP8X4), scales, grouped[:].rearrange("p w t -> p (w t)"))
 
-        def quantise_rows(raw, codes, scales, copy=nc.scalar.copy):
+        def quantise_rows(raw, codes, scales, copy):
             grouped = stage.tile([P, raw.shape[2], PACK], BF16, name="grouped", align_bytes=64)
             interleave(copy, grouped, raw)
             quantise(codes, scales, grouped)
 
-        def quantise_we(half):
+        def quantise_we(half, copy):
             cols = slice(half * WE_HALF, (half + 1) * WE_HALF)
-            quantise_rows(we_raw[half], we_codes[:, cols], we_scales[:, cols], nc.vector.tensor_copy if half in (0,) else nc.scalar.copy)
+            quantise_rows(we_raw[half], we_codes[:, cols], we_scales[:, cols], copy)
 
         def entries(offsets, lo, hi):
             return offsets[:, lo // PER_COLUMN : hi // PER_COLUMN]
 
-        def gather(name, window, offsets, dtype, chunks, bufs):
+        def gather(name, window, offsets, dtype, chunks):
             lo, hi = chunks[0] * CHUNK, (chunks[-1] + 1) * CHUNK
-            dst = work.tile([P, hi - lo], dtype, name=name, bufs=bufs, align_bytes=64)
+            dst = work.tile([P, hi - lo], dtype, name=name, align_bytes=64)
             nc.vector.tensor_copy(dst[:], window.indirect(entries(offsets, lo, hi)))
             for c in chunks:
                 picked[name, c] = dst[:, c * CHUNK - lo : (c + 1) * CHUNK - lo]
 
-        def gather_pass(g, pieces):
-            for chunks in pieces:
-                if g == 1:
-                    gather("scales_a", table_scales[:], list_a, U8, chunks, len(EARLY[g]))
-                for side, offsets in (("a", list_a), ("b", list_b)):
-                    gather("words_%s%d" % (side, g), table[g][:].bitcast(U32), offsets, U32, chunks, len(EARLY[g]))
+        def gather_pass(g, chunks):
+            if g == 1:
+                gather("scales_a", table_scales[:], list_a, U8, chunks)
+            for side, offsets in (("a", list_a), ("b", list_b)):
+                gather("words_%s%d" % (side, g), table[g][:].bitcast(U32), offsets, U32, chunks)
 
-        def first_or_ring(c, shape, dtype, name, bufs=2):
-            if c == 0:
+        def first_or_ring(first, shape, dtype, name, bufs=2):
+            if first:
                 return keep.tile(shape, dtype, name=name + "_first", align_bytes=64)
             return work.tile(shape, dtype, name=name, bufs=bufs, align_bytes=64)
 
@@ -139,37 +142,43 @@ def tile_list_mesh_link_features_kernel(
         load_table(0)
         for q in range(QUADRANTS):
             nc.sync.dma_start(
-                table_scales[32 * q : 32 * q + 4 * PASSES, :].bitcast(I32),
-                tab_scales[:, 4 * q : 4 * q + 4, :].bitcast(I32),
+                table_scales[QUADRANT * q : QUADRANT * q + SCALE_ROWS * PASSES, :].bitcast(I32),
+                tab_scales[:, SCALE_ROWS * q : SCALE_ROWS * (q + 1), :].bitcast(I32),
             )
         wa_raw = [load_rows(wa[0:K_PASS, :])]
         nc.vector.memset(wb_scales_sb[:].rearrange("p g c -> p (g c)").bitcast(I32), 0)
         nc.vector.memset(wc_scales_sb[:].bitcast(I32), 0)
         for g in range(1, PASSES):
             nc.vector.memset(scales_b[g][:].bitcast(I32), 0)
-        for page in pages:
-            nc.vector.memset(page[:].bitcast(I32), 0)
-        gather_pass(0, EARLY[0][:1])
+        nc.vector.memset(minus_anchor[:], -ANCHOR)
+        nc.vector.memset(pages[0][:], 0.0)
+        gather_pass(0, (0, 1))
         nc.vector.tensor_copy(scales_b[0][:], table_scales[:].indirect(list_b[:]))
-        for g in range(1, PASSES):
-            nc.gpsimd.dma_start(scales_b[g][0 : P - 4 * g, :].bitcast(I32), scales_b[0][4 * g : P, :].bitcast(I32))
         wa_raw.append(load_rows(wa[K_PASS : 2 * K_PASS, :]))
         load_table(1)
         wa_raw.append(load_rows(wa[2 * K_PASS : K, :]))
         for q in range(QUADRANTS):
             nc.sync.dma_start(
-                wb_scales_sb[32 * q : 32 * q + 4, :, :].bitcast(I32),
-                wb_scales[:, 4 * q : 4 * q + 4, :].rearrange("g r c -> r g c").bitcast(I32),
+                wb_scales_sb[QUADRANT * q : QUADRANT * q + SCALE_ROWS, :, :].bitcast(I32),
+                wb_scales[:, SCALE_ROWS * q : SCALE_ROWS * (q + 1), :].rearrange("g r c -> r g c").bitcast(I32),
             )
-        load_table(2)
-        nc.sync.dma_start(wb_sb[:].bitcast(I32), wb_words.rearrange("g p c -> p g c").bitcast(I32))
         we_raw = [load_rows(we[:, 0:WE_HALF])]
+        load_table(2)
+        for g in range(1, PASSES):
+            nc.sync.dma_start(
+                scales_b[g][0 : P - SCALE_ROWS * g, :].bitcast(I32), scales_b[0][SCALE_ROWS * g : P, :].bitcast(I32)
+            )
+        nc.sync.dma_start(wb_sb[:].bitcast(I32), wb_words.rearrange("g p c -> p g c").bitcast(I32))
         make_identity(nc, ident[:])
-        nc.vector.memset(minus_anchor[:], -ANCHOR)
+        for page in pages[1:]:
+            nc.gpsimd.memset(page[:], 0.0)
 
-        for g in range(PASSES):
-            quantise_rows(wa_raw[g], wa_codes[g][:], wa_scales[g][:])
-            gather_pass(g, EARLY[g][1 if g == 0 else 0 :])
+        quantise_rows(wa_raw[0], wa_codes[0][:], wa_scales[0][:], nc.scalar.copy)
+        gather_pass(0, (2, 3))
+        for g in range(1, PASSES):
+            quantise_rows(wa_raw[g], wa_codes[g][:], wa_scales[g][:], nc.scalar.copy)
+            gather_pass(g, (0,))
+            gather_pass(g, (1,))
 
         nc.sync.dma_start(gmax_sb[:], gmax.rearrange("(p t) -> p t", t=PACK))
         nc.sync.dma_start(gwave_sb[:], gwave.rearrange("(p t) -> p t", t=PACK))
@@ -177,8 +186,8 @@ def tile_list_mesh_link_features_kernel(
         nc.sync.dma_start(wc_sb[:].bitcast(I32), wc_words[0].bitcast(I32))
         for q in range(QUADRANTS):
             nc.sync.dma_start(
-                wc_scales_sb[32 * q : 32 * q + 4, :].bitcast(I32),
-                wc_scales[0, 4 * q : 4 * q + 4, :].bitcast(I32),
+                wc_scales_sb[QUADRANT * q : QUADRANT * q + SCALE_ROWS, :].bitcast(I32),
+                wc_scales[0, SCALE_ROWS * q : SCALE_ROWS * (q + 1), :].bitcast(I32),
             )
         nc.sync.dma_start(list_out[:], offs3)
         nc.sync.dma_start(wgo_sb[:], wgo)
@@ -188,22 +197,22 @@ def tile_list_mesh_link_features_kernel(
             c, half = divmod(i, 2)
             part = slice(half * BLOCK, (half + 1) * BLOCK)
             cols = slice(i * BLOCK, (i + 1) * BLOCK)
-            a_ps = psum.tile([P, H], F32, name="a_ps", tag="projection", bufs=3)
+            a_ps = psum.tile([P, H], F32, name="a_ps", tag="projection", bufs=2)
             for g in reversed(range(PASSES)):
                 nc.tensor.matmul_mx(
                     a_ps[:], lhsT=picked["words_a%d" % g, c][:, part].bitcast(FP8X4),
-                    lhsT_scale=picked["scales_a", c][4 * g : P, part],
+                    lhsT_scale=picked["scales_a", c][SCALE_ROWS * g : P, part],
                     rhs=wa_codes[g][:].bitcast(FP8X4), rhs_scale=wa_scales[g][:],
                     start=(g == PASSES - 1), stop=(g == 0),
                 )
-            b_ps = psum.tile([P, H], F32, name="b_ps", tag="projection", bufs=3)
+            b_ps = psum.tile([P, H], F32, name="b_ps", tag="projection", bufs=2)
             for g in reversed(range(PASSES)):
                 nc.tensor.matmul_mx(
                     b_ps[:], lhsT=picked["words_b%d" % g, c][:, part].bitcast(FP8X4), lhsT_scale=scales_b[g][:, cols],
                     rhs=wb_sb[:, g, :].bitcast(FP4X4), rhs_scale=wb_scales_sb[:, g, :],
                     start=(g == PASSES - 1), stop=(g == 0),
                 )
-            turns = work.tile([P, 2, PACK, P], F32, name="turns", bufs=2)
+            turns = work.tile([P, 2, PACK, P], F32, name="turns")
             whole = work.tile([P, 2, PACK, P], U32, name="whole")
             for s, (ps, shift) in enumerate(((a_ps, 0.0), (b_ps, QUARTER))):
                 nc.scalar.activation(
@@ -218,13 +227,10 @@ def tile_list_mesh_link_features_kernel(
             turns, whole, larger = angles[i]
             c, half = divmod(i, 2)
             if half == 0:
-                waves[c] = (
-                    work.tile([P, 2, PACK, CHUNK], F32, name="trig"),
-                    work.tile([P, PACK, CHUNK], BF16, name="z1"),
-                )
-            trig = waves[c][0]
+                trig_of[c] = work.tile([P, 2, PACK, CHUNK], F32, name="trig")
+                z1_of[c] = work.tile([P, PACK, CHUNK], BF16, name="z1")
             for s in range(2):
-                reduced = psum.tile([P, PACK, BLOCK], F32, name="reduced", bufs=4)
+                reduced = psum.tile([P, PACK, BLOCK], F32, name="reduced", bufs=REDUCED_BANKS)
                 for t in range(PACK):
                     terms = (whole[:, s, t, :].bitcast(F32), minus_anchor[:], turns[:, s, t, :])
                     for n, term in enumerate(terms):
@@ -233,33 +239,34 @@ def tile_list_mesh_link_features_kernel(
                             start=(n == 0), stop=(n == len(terms) - 1),
                         )
                 nc.scalar.activation(
-                    trig[:, s, :, half * BLOCK : (half + 1) * BLOCK], reduced[:], ACT.Sin, scale=TURN
+                    trig_of[c][:, s, :, half * BLOCK : (half + 1) * BLOCK], reduced[:], ACT.Sin, scale=TURN
                 )
 
         def scale_larger(i):
             larger = angles[i][2]
             c, half = divmod(i, 2)
-            z1 = waves[c][1]
-            larger_ps = psum.tile([P, PACK, BLOCK], F32, name="larger_ps", tag="shared")
+            larger_ps = psum.tile([P, PACK, BLOCK], F32, name="larger_ps", tag=("even_block", "shared")[half])
             for t in range(PACK):
                 nc.tensor.transpose(larger_ps[:, t, :], larger[:, t, :], ident[:])
             for t in range(PACK):
                 nc.scalar.activation(
-                    z1[:, t, half * BLOCK : (half + 1) * BLOCK], larger_ps[:, t, :], ACT.Copy,
+                    z1_of[c][:, t, half * BLOCK : (half + 1) * BLOCK], larger_ps[:, t, :], ACT.Copy,
                     scale=gmax_turn[:, t : t + 1],
                 )
 
-        def features(c):
-            trig, z1 = waves[c]
-            z2 = work.tile([P, PACK, CHUNK], BF16, name="z2")
+        def multiply_waves(c):
+            trig = trig_of[c]
+            z2_of[c] = work.tile([P, PACK, CHUNK], BF16, name="z2")
             for t in range(PACK):
                 nc.vector.scalar_tensor_tensor(
-                    z2[:, t, :], trig[:, 0, t, :], gwave_sb[:, t : t + 1], trig[:, 1, t, :], ALU.mult, ALU.mult
+                    z2_of[c][:, t, :], trig[:, 0, t, :], gwave_sb[:, t : t + 1], trig[:, 1, t, :], ALU.mult, ALU.mult
                 )
-            z1_grouped = first_or_ring(c, [P, CHUNK, PACK], BF16, "z1_grouped")
-            z2_grouped = first_or_ring(c, [P, CHUNK, PACK], BF16, "z2_grouped")
-            interleave(nc.scalar.copy, z1_grouped, z1)
-            interleave(nc.vector.tensor_copy, z2_grouped, z2)
+
+        def quantise_features(c):
+            z1_grouped = first_or_ring(c == 0, [P, CHUNK, PACK], BF16, "z1_grouped")
+            z2_grouped = first_or_ring(c == 0, [P, CHUNK, PACK], BF16, "z2_grouped")
+            interleave(nc.scalar.copy, z1_grouped, z1_of[c])
+            interleave(nc.scalar.copy if 0 < c < LAST else nc.vector.tensor_copy, z2_grouped, z2_of[c])
             z_codes = work.tile([P, 2, CHUNK], U32, name="z_codes", align_bytes=64)
             z_scales = work.tile([P, 2, CHUNK], U8, name="z_scales", align_bytes=64)
             for s, grouped in enumerate((z1_grouped, z2_grouped)):
@@ -292,36 +299,42 @@ def tile_list_mesh_link_features_kernel(
                 nc.sync.dma_start(out[b * P : (b + 1) * P, :], pages[b][:])
 
         def place(c, pair):
-            y = first_or_ring(c + pair, [P, 2, CHUNK], F32, "y", bufs=3)
+            first = c == 0 and pair == 0
+            y = first_or_ring(first, [P, 2, CHUNK], F32, "y", bufs=PAIRS)
             outputs(c, pair, y[:])
             for u in range(2):
                 scatter(2 * pair + u, y[:, u, :], c * CHUNK, (c + 1) * CHUNK)
-            if c + pair == 0:
+            if first:
                 late_page("y")
 
-        slots = [[[], [], [(0, 0)]], [[(0, 1)], [(0, 2)], [(1, 0)]], [[(1, 1)], [(1, 2)], []], [[(2, 0)], [(2, 1)], [(3, 0), (3, 1)]]]
-        quantise_we(0)
+        quantise_we(0, nc.scalar.copy)
         project(0)
         for c in range(CHUNKS):
             project(2 * c + 1)
-            for g in range(PASSES):
-                gather_pass(g, LATE[g][c : c + 1])
-            for pair in slots[c][0]:
-                place(*pair)
             sines(2 * c)
-            sines(2 * c + 1)
-            scale_larger(2 * c)
-            scale_larger(2 * c + 1)
-            features(c)
-            for pair in slots[c][1]:
-                place(*pair)
+            if c > 0:
+                place(c - 1, 0)
             if c < LAST:
                 project(2 * c + 2)
-            for pair in slots[c][2]:
-                place(*pair)
             if c == 0:
-                quantise_we(1)
+                for g in range(1, PASSES):
+                    gather_pass(g, (2, 3))
+            sines(2 * c + 1)
+            multiply_waves(c)
+            if 0 < c < LAST:
+                place(c - 1, 1)
+            scale_larger(2 * c)
+            scale_larger(2 * c + 1)
+            quantise_features(c)
+            if c == 0:
+                quantise_we(1, nc.vector.tensor_copy)
+            elif c < LAST:
+                place(c - 1, LAST_PAIR)
+            else:
+                place(c - 1, 1)
+        for pair in range(LAST_PAIR):
+            place(LAST, pair)
         for d in range(2):
-            outputs(LAST - 1 + d, PAIRS - 1, y_wide[:, :, d, :])
+            outputs(LAST - 1 + d, LAST_PAIR, y_wide[:, :, d, :])
         for u in range(2):
-            scatter(2 * (PAIRS - 1) + u, y_wide[:, u].rearrange("p d j -> p (d j)"), (LAST - 1) * CHUNK, S)
+            scatter(2 * LAST_PAIR + u, y_wide[:, u].rearrange("p d j -> p (d j)"), (LAST - 1) * CHUNK, S)

import math
from contextlib import ExitStack

import concourse.mybir as mybir
from concourse.masks import make_identity

K, H, N, T, S, T2 = 1536, 512, 768, 2048, 1024, 2048
FLOPS = 2 * (2 * K * H * S + 2 * H * N * S)

F32 = mybir.dt.float32
BF16 = mybir.dt.bfloat16
I32 = mybir.dt.int32
U32 = mybir.dt.uint32
U16 = mybir.dt.uint16
U8 = mybir.dt.uint8
FP8X4 = mybir.dt.float8_e4m3fn_x4
FP4X4 = mybir.dt.float4_e2m1fn_x4
ACT = mybir.ActivationFunctionType
ALU = mybir.AluOpType

P = 128
PACK = 4
K_PASS = P * PACK
PASSES = K // K_PASS
QUADRANT = 32
QUADRANTS = P // QUADRANT
SCALE_ROWS = 4
PER_COLUMN = 16
BLOCK = 128
CHUNK = 2 * BLOCK
CHUNKS = S // CHUNK
LAST = CHUNKS - 1
PAGES = N // P
PAIRS = PAGES // 2
LAST_PAIR = PAIRS - 1
WE_HALF = N // 2
EARLY_PAGES = 3
RUN = 4
REDUCED_BANKS = 4

TURN = 2.0 * math.pi
QUARTER = 0.25
ANCHOR = 98304.0
ANCHOR_BITS = 1203765248.0
ULPS_PER_TURN = 128.0


def tile_list_mesh_link_features_kernel(
    tc, tab_words, tab_scales, offs, offs2, offs3, wa, wb_words, wb_scales,
    wc_words, wc_scales, we, gmax, gwave, wgo, out,
):
    nc = tc.nc
    with ExitStack() as ctx:
        keep = ctx.enter_context(tc.tile_pool(name="keep", bufs=1))
        stage = ctx.enter_context(tc.tile_pool(name="stage", bufs=3))
        work = ctx.enter_context(tc.tile_pool(name="work", bufs=2))
        psum = ctx.enter_context(tc.psum_pool(name="psum", bufs=1))

        list_a = keep.tile([P, S // PER_COLUMN], U16, name="list_a")
        list_b = keep.tile([P, S // PER_COLUMN], U16, name="list_b")
        list_out = keep.tile([P, S // PER_COLUMN], U16, name="list_out")
        table = [keep.tile([P, T], I32, name="table%d" % g, align_bytes=64) for g in range(PASSES)]
        table_scales = keep.tile([P, T], U8, name="table_scales", align_bytes=64)
        scales_b = [keep.tile([P, S], U8, name="scales_b%d" % g, align_bytes=64) for g in range(PASSES)]
        wa_codes = [keep.tile([P, H], U32, name="wa_codes%d" % g, align_bytes=64) for g in range(PASSES)]
        wa_scales = [keep.tile([P, H], U8, name="wa_scales%d" % g, align_bytes=64) for g in range(PASSES)]
        wb_sb = keep.tile([P, PASSES, 2 * H], U8, name="wb_sb", align_bytes=64)
        wb_scales_sb = keep.tile([P, PASSES, H], U8, name="wb_scales_sb", align_bytes=64)
        wc_sb = keep.tile([P, 2 * N], U8, name="wc_sb", align_bytes=64)
        wc_scales_sb = keep.tile([P, N], U8, name="wc_scales_sb", align_bytes=64)
        we_codes = keep.tile([P, N], U32, name="we_codes", align_bytes=64)
        we_scales = keep.tile([P, N], U8, name="we_scales", align_bytes=64)
        wgo_sb = keep.tile([P, S], F32, name="wgo_sb")
        gmax_sb = keep.tile([P, PACK], F32, name="gmax_sb")
        gmax_turn = keep.tile([P, PACK], F32, name="gmax_turn")
        gwave_sb = keep.tile([P, PACK], F32, name="gwave_sb")
        ident = keep.tile([P, P], F32, name="ident")
        minus_anchor = keep.tile([P, P], F32, name="minus_anchor")
        warm = keep.tile([P, 2], F32, name="warm")
        y_wide = keep.tile([P, 2, 2, CHUNK], F32, name="y_wide")
        pages = [keep.tile([P, T2], F32, name="page%d" % b) for b in range(EARLY_PAGES)]
        picked, angles, trig_of, z1_of, z2_of, operands = {}, {}, {}, {}, {}, {}

        def load_table(g):
            nc.sync.dma_start(table[g][:], tab_words[g].rearrange("p t i -> p (t i)").bitcast(I32))

        def load_rows(rows):
            raw = stage.tile([P, PACK, rows.shape[1]], F32, name="raw")
            nc.sync.dma_start(raw[:], rows.rearrange("(p t) w -> p t w", t=PACK))
            return raw

        def interleave(copy, grouped, slices):
            copy(
                grouped[:].rearrange("p (c i) t -> p c t i", i=RUN),
                slices[:].rearrange("p t (c i) -> p c t i", i=RUN),
            )

        def quantise(codes, scales, grouped):
            nc.vector.quantize_mx(codes.bitcast(FP8X4), scales, grouped[:].rearrange("p w t -> p (w t)"))

        def quantise_rows(raw, codes, scales, copy):
            grouped = stage.tile([P, raw.shape[2], PACK], BF16, name="grouped", align_bytes=64)
            interleave(copy, grouped, raw)
            quantise(codes, scales, grouped)

        def quantise_we(half, copy):
            cols = slice(half * WE_HALF, (half + 1) * WE_HALF)
            quantise_rows(we_raw[half], we_codes[:, cols], we_scales[:, cols], copy)

        def entries(offsets, lo, hi):
            return offsets[:, lo // PER_COLUMN : hi // PER_COLUMN]

        def gather(name, window, offsets, dtype, chunks):
            lo, hi = chunks[0] * CHUNK, (chunks[-1] + 1) * CHUNK
            dst = work.tile([P, hi - lo], dtype, name=name, align_bytes=64)
            nc.vector.tensor_copy(dst[:], window.indirect(entries(offsets, lo, hi)))
            for c in chunks:
                picked[name, c] = dst[:, c * CHUNK - lo : (c + 1) * CHUNK - lo]

        def gather_pass(g, chunks):
            if g == 1:
                gather("scales_a", table_scales[:], list_a, U8, chunks)
            for side, offsets in (("a", list_a), ("b", list_b)):
                gather("words_%s%d" % (side, g), table[g][:].bitcast(U32), offsets, U32, chunks)

        def first_or_ring(first, shape, dtype, name, bufs=2):
            if first:
                return keep.tile(shape, dtype, name=name + "_first", align_bytes=64)
            return work.tile(shape, dtype, name=name, bufs=bufs, align_bytes=64)

        def late_page(tenant):
            page = keep.tile([P, T2], F32, name="late_page", tag=tenant + "_first", align_bytes=64)
            nc.gpsimd.memset(page[:], 0.0)
            pages.append(page)

        nc.vector.memset(warm[:, 0:1], 0.0)
        nc.scalar.activation(warm[:, 1:2], warm[:, 0:1], ACT.Silu)

        nc.gpsimd.memset(table_scales[:].bitcast(I32), 0)
        nc.sync.dma_start(list_b[:], offs2)
        nc.sync.dma_start(list_a[:], offs)
        load_table(0)
        for q in range(QUADRANTS):
            nc.sync.dma_start(
                table_scales[QUADRANT * q : QUADRANT * q + SCALE_ROWS * PASSES, :].bitcast(I32),
                tab_scales[:, SCALE_ROWS * q : SCALE_ROWS * (q + 1), :].bitcast(I32),
            )
        wa_raw = [load_rows(wa[0:K_PASS, :])]
        nc.vector.memset(wb_scales_sb[:].rearrange("p g c -> p (g c)").bitcast(I32), 0)
        nc.vector.memset(wc_scales_sb[:].bitcast(I32), 0)
        for g in range(1, PASSES):
            nc.vector.memset(scales_b[g][:].bitcast(I32), 0)
        nc.vector.memset(minus_anchor[:], -ANCHOR)
        nc.vector.memset(pages[0][:], 0.0)
        gather_pass(0, (0, 1))
        nc.vector.tensor_copy(scales_b[0][:], table_scales[:].indirect(list_b[:]))
        wa_raw.append(load_rows(wa[K_PASS : 2 * K_PASS, :]))
        load_table(1)
        wa_raw.append(load_rows(wa[2 * K_PASS : K, :]))
        for q in range(QUADRANTS):
            nc.sync.dma_start(
                wb_scales_sb[QUADRANT * q : QUADRANT * q + SCALE_ROWS, :, :].bitcast(I32),
                wb_scales[:, SCALE_ROWS * q : SCALE_ROWS * (q + 1), :].rearrange("g r c -> r g c").bitcast(I32),
            )
        we_raw = [load_rows(we[:, 0:WE_HALF])]
        load_table(2)
        for g in range(1, PASSES):
            nc.sync.dma_start(
                scales_b[g][0 : P - SCALE_ROWS * g, :].bitcast(I32), scales_b[0][SCALE_ROWS * g : P, :].bitcast(I32)
            )
        nc.sync.dma_start(wb_sb[:].bitcast(I32), wb_words.rearrange("g p c -> p g c").bitcast(I32))
        make_identity(nc, ident[:])
        for page in pages[1:]:
            nc.gpsimd.memset(page[:], 0.0)

        quantise_rows(wa_raw[0], wa_codes[0][:], wa_scales[0][:], nc.scalar.copy)
        gather_pass(0, (2, 3))
        for g in range(1, PASSES):
            quantise_rows(wa_raw[g], wa_codes[g][:], wa_scales[g][:], nc.scalar.copy)
            gather_pass(g, (0,))
            gather_pass(g, (1,))

        nc.sync.dma_start(gmax_sb[:], gmax.rearrange("(p t) -> p t", t=PACK))
        nc.sync.dma_start(gwave_sb[:], gwave.rearrange("(p t) -> p t", t=PACK))
        we_raw.append(load_rows(we[:, WE_HALF:N]))
        nc.sync.dma_start(wc_sb[:].bitcast(I32), wc_words[0].bitcast(I32))
        for q in range(QUADRANTS):
            nc.sync.dma_start(
                wc_scales_sb[QUADRANT * q : QUADRANT * q + SCALE_ROWS, :].bitcast(I32),
                wc_scales[0, SCALE_ROWS * q : SCALE_ROWS * (q + 1), :].bitcast(I32),
            )
        nc.sync.dma_start(list_out[:], offs3)
        nc.sync.dma_start(wgo_sb[:], wgo)
        nc.vector.tensor_scalar(gmax_turn[:], gmax_sb[:], TURN, None, ALU.mult)

        def project(i):
            c, half = divmod(i, 2)
            part = slice(half * BLOCK, (half + 1) * BLOCK)
            cols = slice(i * BLOCK, (i + 1) * BLOCK)
            a_ps = psum.tile([P, H], F32, name="a_ps", tag="projection", bufs=2)
            for g in reversed(range(PASSES)):
                nc.tensor.matmul_mx(
                    a_ps[:], lhsT=picked["words_a%d" % g, c][:, part].bitcast(FP8X4),
                    lhsT_scale=picked["scales_a", c][SCALE_ROWS * g : P, part],
                    rhs=wa_codes[g][:].bitcast(FP8X4), rhs_scale=wa_scales[g][:],
                    start=(g == PASSES - 1), stop=(g == 0),
                )
            b_ps = psum.tile([P, H], F32, name="b_ps", tag="projection", bufs=2)
            for g in reversed(range(PASSES)):
                nc.tensor.matmul_mx(
                    b_ps[:], lhsT=picked["words_b%d" % g, c][:, part].bitcast(FP8X4), lhsT_scale=scales_b[g][:, cols],
                    rhs=wb_sb[:, g, :].bitcast(FP4X4), rhs_scale=wb_scales_sb[:, g, :],
                    start=(g == PASSES - 1), stop=(g == 0),
                )
            turns = work.tile([P, 2, PACK, P], F32, name="turns")
            whole = work.tile([P, 2, PACK, P], U32, name="whole")
            for s, (ps, shift) in enumerate(((a_ps, 0.0), (b_ps, QUARTER))):
                nc.scalar.activation(
                    turns[:, s], ps[:].rearrange("p (m t) -> p t m", t=PACK), ACT.Copy, scale=1.0 / TURN, bias=shift
                )
                nc.scalar.activation(whole[:, s], turns[:, s], ACT.Copy, scale=-ULPS_PER_TURN, bias=ANCHOR_BITS)
            larger = work.tile([P, PACK, P], F32, name="larger")
            nc.vector.scalar_tensor_tensor(larger[:], turns[:, 1], -QUARTER, turns[:, 0], ALU.add, ALU.max)
            angles[i] = (turns, whole, larger)

        def sines(i):
            turns, whole, larger = angles[i]
            c, half = divmod(i, 2)
            if half == 0:
                trig_of[c] = work.tile([P, 2, PACK, CHUNK], F32, name="trig")
                z1_of[c] = work.tile([P, PACK, CHUNK], BF16, name="z1")
            for s in range(2):
                reduced = psum.tile([P, PACK, BLOCK], F32, name="reduced", bufs=REDUCED_BANKS)
                for t in range(PACK):
                    terms = (whole[:, s, t, :].bitcast(F32), minus_anchor[:], turns[:, s, t, :])
                    for n, term in enumerate(terms):
                        nc.tensor.matmul(
                            reduced[:, t, :], lhsT=term, rhs=ident[:], is_transpose=True,
                            start=(n == 0), stop=(n == len(terms) - 1),
                        )
                nc.scalar.activation(
                    trig_of[c][:, s, :, half * BLOCK : (half + 1) * BLOCK], reduced[:], ACT.Sin, scale=TURN
                )

        def scale_larger(i):
            larger = angles[i][2]
            c, half = divmod(i, 2)
            larger_ps = psum.tile([P, PACK, BLOCK], F32, name="larger_ps", tag=("even_block", "shared")[half])
            for t in range(PACK):
                nc.tensor.transpose(larger_ps[:, t, :], larger[:, t, :], ident[:])
            for t in range(PACK):
                nc.scalar.activation(
                    z1_of[c][:, t, half * BLOCK : (half + 1) * BLOCK], larger_ps[:, t, :], ACT.Copy,
                    scale=gmax_turn[:, t : t + 1],
                )

        def multiply_waves(c):
            trig = trig_of[c]
            z2_of[c] = work.tile([P, PACK, CHUNK], BF16, name="z2")
            for t in range(PACK):
                nc.vector.scalar_tensor_tensor(
                    z2_of[c][:, t, :], trig[:, 0, t, :], gwave_sb[:, t : t + 1], trig[:, 1, t, :], ALU.mult, ALU.mult
                )

        def quantise_features(c):
            z1_grouped = first_or_ring(c == 0, [P, CHUNK, PACK], BF16, "z1_grouped")
            z2_grouped = first_or_ring(c == 0, [P, CHUNK, PACK], BF16, "z2_grouped")
            interleave(nc.scalar.copy, z1_grouped, z1_of[c])
            interleave(nc.scalar.copy if 0 < c < LAST else nc.vector.tensor_copy, z2_grouped, z2_of[c])
            z_codes = work.tile([P, 2, CHUNK], U32, name="z_codes", align_bytes=64)
            z_scales = work.tile([P, 2, CHUNK], U8, name="z_scales", align_bytes=64)
            for s, grouped in enumerate((z1_grouped, z2_grouped)):
                quantise(z_codes[:, s, :], z_scales[:, s, :], grouped)
            operands[c] = (z_codes, z_scales)
            if c == 0:
                late_page("z2_grouped")
                late_page("z1_grouped")

        def outputs(c, pair, y):
            z_codes, z_scales = operands[c]
            y_ps = psum.tile([P, 2, CHUNK], F32, name="y_ps", tag="shared")
            for u in range(2):
                b = 2 * pair + u
                rows = slice(b * P, (b + 1) * P)
                nc.tensor.matmul_mx(
                    y_ps[:, u, :], lhsT=wc_sb[:, 2 * b * P : 2 * (b + 1) * P].bitcast(FP4X4),
                    lhsT_scale=wc_scales_sb[:, rows], rhs=z_codes[:, 0, :].bitcast(FP8X4),
                    rhs_scale=z_scales[:, 0, :], start=True, stop=False,
                )
                nc.tensor.matmul_mx(
                    y_ps[:, u, :], lhsT=we_codes[:, rows].bitcast(FP8X4), lhsT_scale=we_scales[:, rows],
                    rhs=z_codes[:, 1, :].bitcast(FP8X4), rhs_scale=z_scales[:, 1, :], start=False, stop=True,
                )
            nc.scalar.activation(y, y_ps[:], ACT.Tanh)

        def scatter(b, values, lo, hi):
            nc.vector.tensor_tensor(pages[b][:].indirect(entries(list_out, lo, hi)), values, wgo_sb[:, lo:hi], ALU.mult)
            if hi == S:
                nc.sync.dma_start(out[b * P : (b + 1) * P, :], pages[b][:])

        def place(c, pair):
            first = c == 0 and pair == 0
            y = first_or_ring(first, [P, 2, CHUNK], F32, "y", bufs=PAIRS)
            outputs(c, pair, y[:])
            for u in range(2):
                scatter(2 * pair + u, y[:, u, :], c * CHUNK, (c + 1) * CHUNK)
            if first:
                late_page("y")

        quantise_we(0, nc.scalar.copy)
        project(0)
        for c in range(CHUNKS):
            project(2 * c + 1)
            sines(2 * c)
            if c > 0:
                place(c - 1, 0)
            if c < LAST:
                project(2 * c + 2)
            if c == 0:
                for g in range(1, PASSES):
                    gather_pass(g, (2, 3))
            sines(2 * c + 1)
            multiply_waves(c)
            if 0 < c < LAST:
                place(c - 1, 1)
            scale_larger(2 * c)
            scale_larger(2 * c + 1)
            quantise_features(c)
            if c == 0:
                quantise_we(1, nc.vector.tensor_copy)
            elif c < LAST:
                place(c - 1, LAST_PAIR)
            else:
                place(c - 1, 1)
        for pair in range(LAST_PAIR):
            place(LAST, pair)
        for d in range(2):
            outputs(LAST - 1 + d, LAST_PAIR, y_wide[:, :, d, :])
        for u in range(2):
            scatter(2 * LAST_PAIR + u, y_wide[:, u].rearrange("p d j -> p (d j)"), (LAST - 1) * CHUNK, S)
